import numpy as np
import ml_dtypes


def mxq(x, axis, fmt="e4m3"):
    dtype, down = {"e4m3": (ml_dtypes.float8_e4m3fn, 7), "e5m2": (ml_dtypes.float8_e5m2, 14)}[fmt]
    v = np.moveaxis(np.asarray(x, np.float32).astype(ml_dtypes.bfloat16).astype(np.float64), axis, -1)
    blocks = v.reshape(v.shape[:-1] + (-1, 32))
    amax = np.abs(blocks).max(-1, keepdims=True)
    byte = np.maximum(np.where(amax > 0, np.frexp(amax)[1] - 1 + 127, 0) - down, 1)
    scale = np.exp2(byte - 127.0)
    codes = (blocks / scale).astype(np.float32).astype(dtype).astype(np.float64)
    return np.moveaxis((codes * scale).reshape(v.shape), -1, axis)


WIDE = False


def mx_kscale(k):
    if not WIDE:
        return np.ones(k)
    levels = np.array([10, -10, 5, -5, 0])
    if k % 512:
        return np.exp2(np.random.permutation(np.resize(levels, k // 32))).repeat(32)
    a = np.empty((k // 512, 16))
    for p in range(k // 512):
        a[p, :8] = np.random.permutation(np.resize(levels, 8))
        for g in range(8):
            far = levels[np.abs(levels - a[p, g]) >= 10]
            a[p, g + 8] = far[np.random.randint(len(far))]
    return np.exp2(a.ravel()).repeat(32)


BF16 = ml_dtypes.bfloat16


def bf(x):
    return np.asarray(x, np.float32).astype(BF16)


def f64(x):
    return np.asarray(x).astype(np.float64)


E2M1 = np.array([0.0, 0.5, 1.0, 1.5, 2.0, 3.0, 4.0, 6.0, -0.0, -0.5, -1.0, -1.5, -2.0, -3.0, -4.0, -6.0])


def pack_weight(w, fmt):
    k, n = w.shape
    w = f64(bf(w)).reshape(k // 32, 32, n)
    amax = np.abs(w).max(1)
    if fmt == "e4m3":
        byte = np.frexp(amax)[1] - 1 + 127 - 7
    else:
        mant, ex = np.frexp(amax / 6.0)
        byte = np.where(mant > 0.5, ex, ex - 1) + 127
    byte = np.clip(np.where(amax > 0, byte, 1), 1, 254)
    scaled = (w * np.exp2(127.0 - byte)[:, None, :]).reshape(k, n).astype(np.float32)
    by_word = np.ascontiguousarray(scaled.reshape(k // 512, 128, 4, n).transpose(0, 1, 3, 2))
    if fmt == "e4m3":
        words = by_word.astype(ml_dtypes.float8_e4m3fn).view(np.uint8)
    else:
        c = by_word.astype(ml_dtypes.float4_e2m1fn).view(np.uint8) & 0xF
        words = c[..., 0::2] | (c[..., 1::2] << 4)
    return np.ascontiguousarray(words), np.ascontiguousarray(byte.astype(np.uint8).reshape(k // 512, 16, n))


def unpack_weight(words, scales, fmt):
    g, p, n, _ = words.shape
    if fmt == "e4m3":
        vals = np.ascontiguousarray(words).view(ml_dtypes.float8_e4m3fn).astype(np.float64)
    else:
        nib = np.empty((g, p, n, 4), np.uint8)
        nib[..., 0::2] = words & 0xF
        nib[..., 1::2] = words >> 4
        vals = E2M1[nib]
    vals = vals * np.repeat(np.exp2(scales.astype(np.float64) - 127.0), 8, axis=1)[..., None]
    return vals.transpose(0, 1, 3, 2).reshape(g * 512, n)
def pack4(w):
    words, scales = pack_weight(w, "e2m1")
    return words.reshape(words.shape[0], 128, -1), scales


def unpack4(words, scales):
    return unpack_weight(words.reshape(words.shape[0], 128, -1, 2), scales, "e2m1")


def planes(Y):
    n, m = Y.shape
    b = f64(bf(Y)).reshape(n // 32, 32, m)
    amax = np.abs(b).max(1)
    byte = np.clip(np.where(amax > 0, np.frexp(amax)[1] - 1 + 127 - 7, 1), 1, 254)
    codes = (b * np.exp2(127.0 - byte)[:, None, :]).reshape(n, m).astype(np.float32).astype(ml_dtypes.float8_e4m3fn).view(np.uint8)
    words = codes.reshape(n // 512, 128, 4, m).transpose(0, 1, 3, 2)
    return np.ascontiguousarray(words), np.ascontiguousarray(byte.astype(np.uint8).reshape(n // 512, 16, m))


B, T, D, C = 4, 512, 1536, 1024

PAST = 0.25


def setup_inputs():
    s = mx_kscale(D)
    x = np.random.randn(B * T, D) * s
    x_words, x_scales = pack_weight(x.T, "e4m3")
    spread = np.exp(0.8 * np.random.randn(C))
    w_key = np.random.randn(D, C) / np.sqrt(D) * spread / s[:, None]
    pad_key = np.random.randn(C) * spread
    lengths = np.random.randint(T // 4, T - T // 4, size=(B, 1))
    mask = np.where(np.arange(T)[None, :] < lengths, 1.0, PAST)
    return {"x_words": x_words, "x_scales": x_scales, "w_key": bf(w_key),
            "mask": bf(mask), "pad_key": bf(pad_key)}


def reference(x_words, x_scales, w_key, mask, pad_key):
    xt = unpack_weight(x_words, x_scales, "e4m3")
    h = (xt.T @ mxq(f64(w_key), 0, "e4m3")).reshape(B, T, C)
    keep = f64(mask)[:, :, None]
    y = keep * h + (1.0 - keep) * f64(pad_key)
    Y = y.reshape(B * T, C).T
    words, scales = planes(Y)
    return y, words, scales

@@ -1,0 +1,353 @@
+from contextlib import ExitStack
+
+import concourse.mybir as mybir
+from concourse.masks import make_identity
+
+F32 = mybir.dt.float32
+BF16 = mybir.dt.bfloat16
+I32 = mybir.dt.int32
+U32 = mybir.dt.uint32
+U8 = mybir.dt.uint8
+FP8X4 = mybir.dt.float8_e4m3fn_x4
+ALU = mybir.AluOpType
+ACT = mybir.ActivationFunctionType
+
+P = 128
+TOKENS, D, C = 2048, 1536, 1024
+PASSES = D // 512
+HALF = 512
+TILES = TOKENS // P
+UNITS = 2 * TILES
+BATCH = 4
+CHUNK = BATCH * P
+LAG = 3
+Q_AHEAD = 12
+Q_HEAD = 12
+X_BOUNDS = [0,6,10,13,16]
+FIRST = X_BOUNDS[1]
+W1_VECTOR = [[3,0,0,256],[4,0,256,512],[6,1,0,256],[8,2,0,256]]
+W1_SCALAR = [[5,1,256,512],[7,2,256,512]]
+W1_QUANT = [[5,0],[7,1],[9,2]]
+HEAD_SPLIT = 512
+QLAG = 2
+
+AHEAD = 2
+TURN_AT = [8,12,15,19,22,26,29]
+UNLOAD_A = [4,8,12,17,21,25,27]
+UNLOAD_B = [5,9,13,18,22,26,28]
+QUANT_AT = [12,14,16,21,25,28]
+
+FLOPS = 2 * TOKENS * D * C
+
+
+def tile_length_masked_cross_keys_g6_kernel(tc, x_words, x_scales, w_key, mask, pad_key, out_0, out_1, out_2):
+    nc = tc.nc
+    y_rows = out_0.rearrange("b t c -> (b t) c")
+
+    with ExitStack() as ctx:
+        keep = ctx.enter_context(tc.tile_pool(name="keep", bufs=1))
+        flow = ctx.enter_context(tc.tile_pool(name="flow", bufs=1))
+        psum = ctx.enter_context(tc.psum_pool(name="psum", bufs=1))
+        ctx.enter_context(tc.manual_schedule())
+
+        w_raw = {}
+        w_grouped = {}
+        w_codes = {}
+        w_scales = {}
+        x_codes = {}
+        q_tiles = {}
+        acc = {}
+        y_tiles = {}
+        y_bf = {}
+        turned = {}
+        y_grouped = {}
+
+        def load_w(g, h):
+            w_raw[g, h] = keep.tile([P, 4, HALF], BF16, name="w_raw_%d_%d" % (g, h), align_bytes=64)
+            rows = w_key[512 * g : 512 * (g + 1), HALF * h : HALF * (h + 1)]
+            nc.sync.dma_start(out=w_raw[g, h][:], in_=rows.rearrange("(p j) c -> p j c", j=4))
+
+        def x_view(g):
+            return x_words[g].rearrange("p n t -> p (n t)").bitcast(I32)
+
+        def load_x_first(g):
+            t = keep.tile([P, P * FIRST], U32, name="x_first_%d" % g, align_bytes=64)
+            nc.sync.dma_start(out=t[:].bitcast(I32), in_=x_view(g)[:, 0 : P * FIRST])
+            for i in range(FIRST):
+                x_codes[g, i] = t[:, P * i : P * (i + 1)]
+
+        def load_x(k):
+            i0, i1 = X_BOUNDS[k], X_BOUNDS[k + 1]
+            t = keep.tile([P, PASSES, P * (i1 - i0)], U32, name="x_chunk_%d" % k, align_bytes=64)
+            src = x_words.rearrange("g p n t -> p g (n t)").bitcast(I32)
+            nc.sync.dma_start(out=t[:].bitcast(I32), in_=src[:, :, P * i0 : P * i1])
+            for g in range(PASSES):
+                for i in range(i0, i1):
+                    x_codes[g, i] = t[:, g, P * (i - i0) : P * (i - i0 + 1)]
+
+        def load_x_scales(plane, n0, n1):
+            for quad in range(4):
+                src = x_scales[:, 4 * quad : 4 * quad + 4, n0:n1].rearrange("g r n -> r g n")
+                nc.sync.dma_start(out=plane[32 * quad : 32 * quad + 4, :, :].bitcast(I32), in_=src.bitcast(I32))
+
+        def interleave_w(g, h, c0, c1, on_scalar):
+            if (g, h) not in w_grouped:
+                w_grouped[g, h] = flow.tile([P, 4 * HALF], BF16, name="w_grouped", tag="w_grouped", bufs=3, align_bytes=64)
+            dst = w_grouped[g, h][:, 4 * c0 : 4 * c1].rearrange("p (c i t) -> p c t i", i=4, t=4)
+            src = w_raw[g, h][:, :, c0:c1].rearrange("p t (c i) -> p c t i", i=4)
+            if on_scalar:
+                nc.scalar.copy(out=dst, in_=src)
+            else:
+                nc.vector.tensor_copy(out=dst, in_=src)
+
+        def quantize_w(g, h, c0, c1):
+            if c0 == 0:
+                w_codes[g, h] = keep.tile([P, HALF], U32, name="w_codes_%d_%d" % (g, h), align_bytes=64)
+                w_scales[g, h] = keep.tile([P, HALF], U8, name="w_scales_%d_%d" % (g, h), align_bytes=64)
+            nc.vector.quantize_mx(
+                out=w_codes[g, h][:, c0:c1].bitcast(FP8X4),
+                scales=w_scales[g, h][:, c0:c1],
+                in_=w_grouped[g, h][:, 4 * c0 : 4 * c1],
+            )
+
+        def make_q(u, on_scalar):
+            h, i = divmod(u, TILES)
+            if BATCH <= u < Q_AHEAD:
+                q_tiles[u] = keep.tile([P, HALF], F32, name="q_%d" % u, align_bytes=64)
+            else:
+                q_tiles[u] = flow.tile([P, HALF], F32, name="q", tag="q", bufs=BATCH, align_bytes=64)
+            src = pad_rows[:, HALF * h : HALF * (h + 1)]
+            if on_scalar:
+                nc.scalar.activation(out=q_tiles[u][:], in_=src, func=ACT.Copy, scale=rest[:, i : i + 1])
+            else:
+                nc.gpsimd.tensor_scalar(
+                    out=q_tiles[u][:], in0=src, scalar1=rest[:, i : i + 1], scalar2=1.0, op0=ALU.mult, op1=ALU.mult
+                )
+
+        def mx_pass(u, g):
+            h, i = divmod(u, TILES)
+            if g == 0:
+                acc[u] = psum.tile([P, HALF], F32, name="acc", tag="acc", bufs=6)
+            if i < FIRST:
+                plane = xs_first[:, g, P * i : P * (i + 1)]
+            else:
+                plane = xs_rest[:, g, P * (i - FIRST) : P * (i - FIRST + 1)]
+            nc.tensor.matmul_mx(
+                out=acc[u][:],
+                lhsT=x_codes[g, i].bitcast(FP8X4),
+                lhsT_scale=plane,
+                rhs=w_codes[g, h][:].bitcast(FP8X4),
+                rhs_scale=w_scales[g, h][:],
+                start=(g == 0),
+                stop=(g == PASSES - 1),
+            )
+
+        def blend(u):
+            h, i = divmod(u, TILES)
+            if u % 2 == 0:
+                y_tiles[u // 2] = flow.tile([P, 2, HALF], F32, name="y", tag="y", bufs=12, align_bytes=64)
+            nc.vector.scalar_tensor_tensor(
+                out=y_tiles[u // 2][:, u % 2, :],
+                in0=acc[u][:],
+                scalar=keep_m[:, i : i + 1],
+                in1=q_tiles[u][:],
+                op0=ALU.mult,
+                op1=ALU.add,
+            )
+
+        def store_y(u0, u1):
+            h, i = divmod(u0, TILES)
+            n = u1 - u0
+            dst = y_rows[P * i : P * (i + n), HALF * h : HALF * (h + 1)].rearrange("(i p) c -> p i c", p=P)
+            nc.sync.dma_start(out=dst, in_=y_tiles[u0 // 2][:, u0 % 2 : u0 % 2 + n, :])
+
+        def round_y(u):
+            y_bf[u] = flow.tile([P, HALF], BF16, name="y_bf", tag="y_bf", bufs=8, align_bytes=64)
+            nc.scalar.copy(
+                out=y_bf[u][:].rearrange("p (s c e) -> p s c e", s=2, e=2),
+                in_=y_tiles[u // 2][:, u % 2, :].rearrange("p (c s e) -> p s c e", s=2, e=2),
+            )
+
+        def blend_rounded(u):
+            h, i = divmod(u, TILES)
+            y_bf[u] = flow.tile([P, HALF], BF16, name="y_bf", tag="y_bf", bufs=8, align_bytes=64)
+            for s in range(2):
+                nc.vector.scalar_tensor_tensor(
+                    out=y_bf[u][:, 2 * P * s : 2 * P * (s + 1)].rearrange("p (c e) -> p c e", e=2),
+                    in0=acc[u][:].rearrange("p (c s e) -> p s c e", s=2, e=2)[:, s],
+                    scalar=keep_m[:, i : i + 1],
+                    in1=q_tiles[u][:].rearrange("p (c s e) -> p s c e", s=2, e=2)[:, s],
+                    op0=ALU.mult,
+                    op1=ALU.add,
+                )
+
+        def turn(u0, n, tag, bufs):
+            bank = psum.tile([P, n, 2, P], F32, name="turned", tag=tag, bufs=bufs)
+            turned[u0] = bank
+            for a in range(n):
+                words = y_bf[u0 + a][:].bitcast(F32)
+                for s in range(2):
+                    nc.tensor.transpose(bank[:, a, s, :], words[:, P * s : P * (s + 1)], ident_f32[:])
+
+        def unload(u0, n):
+            b, j = divmod(u0, BATCH)
+            if j == 0:
+                y_grouped[b] = flow.tile([P, 4 * CHUNK], BF16, name="y_grouped", tag="y_grouped", bufs=4, align_bytes=64)
+            dst = y_grouped[b][:, 4 * P * j : 4 * P * (j + n)].bitcast(F32)
+            nc.scalar.copy(
+                out=dst.rearrange("p (a m s) -> p a m s", a=n, s=2),
+                in_=turned[u0][:].rearrange("p a s m -> p a m s"),
+            )
+
+        def quantize_y(u0, n):
+            h, i = divmod(u0, TILES)
+            b, j = divmod(u0, BATCH)
+            nc.vector.quantize_mx(
+                out=y_codes[h][:, P * i : P * (i + n)].bitcast(FP8X4),
+                scales=y_scales[h][:, P * i : P * (i + n)],
+                in_=y_grouped[b][:, 4 * P * j : 4 * P * (j + n)],
+            )
+
+        def store_codes(u0, n, queue):
+            h, i = divmod(u0, TILES)
+            dst = out_1[h].rearrange("p n t -> p (n t)").bitcast(I32)
+            queue.dma_start(out=dst[:, P * i : P * (i + n)], in_=y_codes[h][:, P * i : P * (i + n)].bitcast(I32))
+
+        def store_scales(h, queues):
+            for quad in range(4):
+                queues[quad % len(queues)].dma_start(
+                    out=out_2[h, 4 * quad : 4 * quad + 4, :].bitcast(I32),
+                    in_=y_scales[h][32 * quad : 32 * quad + 4, :].bitcast(I32),
+                )
+
+        xs_first = keep.tile([P, PASSES, P * FIRST], U8, align_bytes=64)
+        xs_rest = keep.tile([P, PASSES, TOKENS - P * FIRST], U8, align_bytes=64)
+        mask_rows = keep.tile([P, P], BF16, align_bytes=64)
+        pad_cols = keep.tile([P, 2, 4], BF16, align_bytes=64)
+        ident_bf = keep.tile([P, P], BF16, align_bytes=64)
+        ident_f32 = keep.tile([P, P], F32, align_bytes=64)
+        keep_m = keep.tile([P, TILES], F32, align_bytes=64)
+        rest = keep.tile([P, TILES], F32, align_bytes=64)
+        pad_rows = keep.tile([P, C], F32, align_bytes=64)
+        y_codes = [keep.tile([P, TOKENS], U32, name="y_codes_%d" % h, align_bytes=64) for h in range(2)]
+        y_scales = [keep.tile([P, TOKENS], U8, name="y_scales_%d" % h, align_bytes=64) for h in range(2)]
+
+        nc.vector.memset(mask_rows[:], 0.0)
+        nc.vector.memset(xs_first[:].bitcast(U32), 0)
+        nc.vector.memset(xs_rest[:].bitcast(U32), 0)
+        make_identity(nc, ident_bf[:])
+        make_identity(nc, ident_f32[:])
+
+        load_w(0, 0)
+        nc.scalar.dma_start(out=pad_cols[:], in_=pad_key.rearrange("(h p j) -> p h j", h=2, j=4))
+        nc.scalar.dma_start(out=mask_rows[0:TILES, :], in_=mask.rearrange("b (i p) -> (b i) p", p=P))
+        load_x_scales(xs_first, 0, P * FIRST)
+        load_x_first(0)
+        load_w(1, 0)
+        load_x_first(1)
+        load_w(2, 0)
+        load_x_first(2)
+        load_x_scales(xs_rest, P * FIRST, TOKENS)
+        load_x(1)
+        load_w(0, 1)
+        load_x(2)
+        load_w(1, 1)
+        load_w(2, 1)
+        load_x(3)
+
+        mask_bank = psum.tile([P, P], BF16, name="mask_bank", tag="turned", bufs=2)
+        nc.tensor.transpose(mask_bank[:], mask_rows[:], ident_bf[:])
+        pad_bank = psum.tile([P, 2, 4, P], BF16, name="pad_bank", tag="turned", bufs=2)
+        for h in range(2):
+            for j in range(4):
+                nc.tensor.transpose(pad_bank[:, h, j, :], pad_cols[:, h, j : j + 1].to_broadcast([P, P]), ident_bf[:])
+        nc.scalar.activation(out=rest[:], in_=mask_bank[:, 0:TILES], func=ACT.Copy, scale=-1.0, bias=1.0)
+        nc.scalar.activation(out=keep_m[:], in_=mask_bank[:, 0:TILES], func=ACT.Copy)
+
+        def spread_pad(h):
+            nc.scalar.activation(
+                out=pad_rows[:, HALF * h : HALF * (h + 1)].rearrange("p (n j) -> p n j", j=4),
+                in_=pad_bank[:, h, :, :].rearrange("p j n -> p n j"),
+                func=ACT.Copy,
+            )
+
+        spread_pad(0)
+        for u in range(Q_HEAD):
+            make_q(u, True)
+        for g in range(PASSES):
+            if g == PASSES - 1 and HEAD_SPLIT < HALF:
+                interleave_w(g, 0, 0, HALF // 2, False)
+                interleave_w(g, 0, HALF // 2, HEAD_SPLIT, False)
+                interleave_w(g, 0, HEAD_SPLIT, HALF, True)
+            else:
+                interleave_w(g, 0, 0, HALF // 2, False)
+                interleave_w(g, 0, HALF // 2, HALF, False)
+            quantize_w(g, 0, 0, HALF // 2)
+            quantize_w(g, 0, HALF // 2, HALF)
+            for u in range(FIRST):
+                mx_pass(u, g)
+        for u in range(Q_HEAD, Q_AHEAD):
+            make_q(u, True)
+        spread_pad(1)
+
+        last = UNITS - 1
+        for u in range(UNITS):
+            if u == last:
+                blend_rounded(u)
+            blend(u)
+            if u < BATCH:
+                make_q(u + Q_AHEAD, False)
+            elif Q_AHEAD <= u < UNITS - BATCH:
+                make_q(u + BATCH, False)
+            if u < last:
+                round_y(u)
+            ahead = u + 4 if u + 4 < TILES else (u + AHEAD if u + AHEAD >= TILES else -1)
+            if FIRST <= ahead < UNITS:
+                for g in range(PASSES):
+                    mx_pass(ahead, g)
+            if ahead in TURN_AT:
+                b = TURN_AT.index(ahead)
+                turn(BATCH * b, 2, "turned", 2)
+                turn(BATCH * b + 2, 2, "turned", 2)
+            if u in UNLOAD_A:
+                unload(BATCH * UNLOAD_A.index(u), 2)
+            if u in UNLOAD_B:
+                unload(BATCH * UNLOAD_B.index(u) + 2, 2)
+            if u % 2 == 1 and u < last:
+                store_y(u - 1, u + 1)
+            if u >= last - 1:
+                store_y(u, u + 1)
+            for at, g, c0, c1 in W1_SCALAR:
+                if at == u:
+                    interleave_w(g, 1, c0, c1, True)
+            for at, g, c0, c1 in W1_VECTOR:
+                if at == u:
+                    interleave_w(g, 1, c0, c1, False)
+            for at, g in W1_QUANT:
+                if at == u:
+                    quantize_w(g, 1, 0, HALF)
+            if u in QUANT_AT:
+                b = QUANT_AT.index(u)
+                quantize_y(BATCH * b, BATCH)
+                store_codes(BATCH * b, BATCH, nc.sync)
+                if BATCH * (b + 1) == TILES:
+                    store_scales(0, [nc.sync])
+            if u == last - 2:
+                quantize_y(UNITS - 2 * BATCH, 2)
+            if u == last - 1:
+                quantize_y(UNITS - 2 * BATCH + 2, 2)
+                store_codes(UNITS - 2 * BATCH, BATCH, nc.sync)
+
+        u0 = UNITS - BATCH
+        turn(u0, 2, "turned", 2)
+        turn(u0 + 2, 1, "turned", 2)
+        turn(u0 + 3, 1, "acc", 6)
+        unload(u0, 2)
+        unload(u0 + 2, 1)
+        unload(u0 + 3, 1)
+        quantize_y(u0, 2)
+        quantize_y(u0 + 2, 1)
+        store_codes(u0, 2, nc.sync)
+        quantize_y(u0 + 3, 1)
+        store_codes(u0 + 2, 2, nc.sync)
+        store_scales(1, [nc.scalar, nc.sync])

@@ -21,21 +21,25 @@ UNITS = 2 * TILES
 BATCH = 4
 CHUNK = BATCH * P
 LAG = 3
-Q_AHEAD = 12
-Q_HEAD = 12
-X_BOUNDS = [0,6,10,13,16]
+Q_AHEAD = 10
+Q_BEFORE = [0,0,0,5]
+X_BOUNDS = [0,5,9,13,16]
 FIRST = X_BOUNDS[1]
-W1_VECTOR = [[3,0,0,256],[4,0,256,512],[6,1,0,256],[8,2,0,256]]
-W1_SCALAR = [[5,1,256,512],[7,2,256,512]]
-W1_QUANT = [[5,0],[7,1],[9,2]]
+W1_VECTOR = [[6,0,256,512],[8,1,0,256],[10,2,0,256]]
+W1_SCALAR = [[2,0,0,256],[5,1,256,512],[8,2,256,512]]
+W1_QUANT = [[7,0],[9,1],[11,2]]
 HEAD_SPLIT = 512
 QLAG = 2
 
 AHEAD = 2
-TURN_AT = [8,12,15,19,22,26,29]
-UNLOAD_A = [4,8,12,17,21,25,27]
-UNLOAD_B = [5,9,13,18,22,26,28]
-QUANT_AT = [12,14,16,21,25,28]
+AHEAD0 = 3
+SWITCH = 22
+TURN_AT = [8,12,16,20,23,26,29]
+UNLOAD_A = [5,9,13,17,21,24,27]
+UNLOAD_B = [6,10,14,18,21,24,27]
+QUANT_AT = [9,13,17,21,24,27]
+
+SCALE_CUT = 8
 
 FLOPS = 2 * TOKENS * D * C
 
@@ -85,11 +89,6 @@ def tile_length_masked_cross_keys_g6_kernel(tc, x_words, x_scales, w_key, mask, 
                 for i in range(i0, i1):
                     x_codes[g, i] = t[:, g, P * (i - i0) : P * (i - i0 + 1)]
 
-        def load_x_scales(plane, n0, n1):
-            for quad in range(4):
-                src = x_scales[:, 4 * quad : 4 * quad + 4, n0:n1].rearrange("g r n -> r g n")
-                nc.sync.dma_start(out=plane[32 * quad : 32 * quad + 4, :, :].bitcast(I32), in_=src.bitcast(I32))
-
         def interleave_w(g, h, c0, c1, on_scalar):
             if (g, h) not in w_grouped:
                 w_grouped[g, h] = flow.tile([P, 4 * HALF], BF16, name="w_grouped", tag="w_grouped", bufs=3, align_bytes=64)
@@ -131,7 +130,7 @@ def tile_length_masked_cross_keys_g6_kernel(tc, x_words, x_scales, w_key, mask, 
             if i < FIRST:
                 plane = xs_first[:, g, P * i : P * (i + 1)]
             else:
-                plane = xs_rest[:, g, P * (i - FIRST) : P * (i - FIRST + 1)]
+                plane = x_planes[4 * g : P, P * (i - FIRST) : P * (i - FIRST + 1)]
             nc.tensor.matmul_mx(
                 out=acc[u][:],
                 lhsT=x_codes[g, i].bitcast(FP8X4),
@@ -162,7 +161,7 @@ def tile_length_masked_cross_keys_g6_kernel(tc, x_words, x_scales, w_key, mask, 
             nc.sync.dma_start(out=dst, in_=y_tiles[u0 // 2][:, u0 % 2 : u0 % 2 + n, :])
 
         def round_y(u):
-            y_bf[u] = flow.tile([P, HALF], BF16, name="y_bf", tag="y_bf", bufs=8, align_bytes=64)
+            y_bf[u] = flow.tile([P, HALF], BF16, name="y_bf", tag="y_bf", bufs=12, align_bytes=64)
             nc.scalar.copy(
                 out=y_bf[u][:].rearrange("p (s c e) -> p s c e", s=2, e=2),
                 in_=y_tiles[u // 2][:, u % 2, :].rearrange("p (c s e) -> p s c e", s=2, e=2),
@@ -170,7 +169,7 @@ def tile_length_masked_cross_keys_g6_kernel(tc, x_words, x_scales, w_key, mask, 
 
         def blend_rounded(u):
             h, i = divmod(u, TILES)
-            y_bf[u] = flow.tile([P, HALF], BF16, name="y_bf", tag="y_bf", bufs=8, align_bytes=64)
+            y_bf[u] = flow.tile([P, HALF], BF16, name="y_bf", tag="y_bf", bufs=12, align_bytes=64)
             for s in range(2):
                 nc.vector.scalar_tensor_tensor(
                     out=y_bf[u][:, 2 * P * s : 2 * P * (s + 1)].rearrange("p (c e) -> p c e", e=2),
@@ -202,9 +201,11 @@ def tile_length_masked_cross_keys_g6_kernel(tc, x_words, x_scales, w_key, mask, 
         def quantize_y(u0, n):
             h, i = divmod(u0, TILES)
             b, j = divmod(u0, BATCH)
+            i0 = SCALE_CUT if h == 1 and i >= SCALE_CUT else 0
+            plane = y_scales[h, i0][:, P * (i - i0) : P * (i - i0 + n)]
             nc.vector.quantize_mx(
                 out=y_codes[h][:, P * i : P * (i + n)].bitcast(FP8X4),
-                scales=y_scales[h][:, P * i : P * (i + n)],
+                scales=plane,
                 in_=y_grouped[b][:, 4 * P * j : 4 * P * (j + n)],
             )
 
@@ -213,15 +214,16 @@ def tile_length_masked_cross_keys_g6_kernel(tc, x_words, x_scales, w_key, mask, 
             dst = out_1[h].rearrange("p n t -> p (n t)").bitcast(I32)
             queue.dma_start(out=dst[:, P * i : P * (i + n)], in_=y_codes[h][:, P * i : P * (i + n)].bitcast(I32))
 
-        def store_scales(h, queues):
+        def store_scales(h, i0, queues):
+            tile = y_scales[h, i0]
             for quad in range(4):
                 queues[quad % len(queues)].dma_start(
-                    out=out_2[h, 4 * quad : 4 * quad + 4, :].bitcast(I32),
-                    in_=y_scales[h][32 * quad : 32 * quad + 4, :].bitcast(I32),
+                    out=out_2[h, 4 * quad : 4 * quad + 4, P * i0 : P * i0 + tile.shape[1]].bitcast(I32),
+                    in_=tile[32 * quad : 32 * quad + 4, :].bitcast(I32),
                 )
 
         xs_first = keep.tile([P, PASSES, P * FIRST], U8, align_bytes=64)
-        xs_rest = keep.tile([P, PASSES, TOKENS - P * FIRST], U8, align_bytes=64)
+        x_planes = keep.tile([P, TOKENS - P * FIRST], U8, align_bytes=64)
         mask_rows = keep.tile([P, P], BF16, align_bytes=64)
         pad_cols = keep.tile([P, 2, 4], BF16, align_bytes=64)
         ident_bf = keep.tile([P, P], BF16, align_bytes=64)
@@ -230,24 +232,31 @@ def tile_length_masked_cross_keys_g6_kernel(tc, x_words, x_scales, w_key, mask, 
         rest = keep.tile([P, TILES], F32, align_bytes=64)
         pad_rows = keep.tile([P, C], F32, align_bytes=64)
         y_codes = [keep.tile([P, TOKENS], U32, name="y_codes_%d" % h, align_bytes=64) for h in range(2)]
-        y_scales = [keep.tile([P, TOKENS], U8, name="y_scales_%d" % h, align_bytes=64) for h in range(2)]
+        y_scales = {}
+        for h, i0, i1 in ((0, 0, TILES), (1, 0, SCALE_CUT), (1, SCALE_CUT, TILES)):
+            y_scales[h, i0] = keep.tile([P, P * (i1 - i0)], U8, name="y_scales_%d_%d" % (h, i0), align_bytes=64)
 
         nc.vector.memset(mask_rows[:], 0.0)
         nc.vector.memset(xs_first[:].bitcast(U32), 0)
-        nc.vector.memset(xs_rest[:].bitcast(U32), 0)
+        nc.vector.memset(x_planes[:].bitcast(U32), 0)
         make_identity(nc, ident_bf[:])
-        make_identity(nc, ident_f32[:])
+        nc.gpsimd.dma_start(out=mask_rows[0:TILES, :], in_=mask.rearrange("b (i p) -> (b i) p", p=P))
+        for quad in (0, 2, 1, 3):
+            nc.gpsimd.dma_start(
+                out=x_planes[32 * quad : 32 * quad + 4 * PASSES, :].bitcast(I32),
+                in_=x_scales[:, 4 * quad : 4 * quad + 4, P * FIRST : TOKENS].bitcast(I32),
+            )
 
         load_w(0, 0)
         nc.scalar.dma_start(out=pad_cols[:], in_=pad_key.rearrange("(h p j) -> p h j", h=2, j=4))
-        nc.scalar.dma_start(out=mask_rows[0:TILES, :], in_=mask.rearrange("b (i p) -> (b i) p", p=P))
-        load_x_scales(xs_first, 0, P * FIRST)
+        for quad in (0, 2, 1, 3):
+            src = x_scales[:, 4 * quad : 4 * quad + 4, 0 : P * FIRST].rearrange("g r n -> r g n")
+            nc.sync.dma_start(out=xs_first[32 * quad : 32 * quad + 4, :, :].bitcast(I32), in_=src.bitcast(I32))
         load_x_first(0)
         load_w(1, 0)
-        load_x_first(1)
         load_w(2, 0)
+        load_x_first(1)
         load_x_first(2)
-        load_x_scales(xs_rest, P * FIRST, TOKENS)
         load_x(1)
         load_w(0, 1)
         load_x(2)
@@ -255,14 +264,13 @@ def tile_length_masked_cross_keys_g6_kernel(tc, x_words, x_scales, w_key, mask, 
         load_w(2, 1)
         load_x(3)
 
-        mask_bank = psum.tile([P, P], BF16, name="mask_bank", tag="turned", bufs=2)
-        nc.tensor.transpose(mask_bank[:], mask_rows[:], ident_bf[:])
+        nc.scalar.activation(out=ident_f32[:], in_=ident_bf[:], func=ACT.Copy)
         pad_bank = psum.tile([P, 2, 4, P], BF16, name="pad_bank", tag="turned", bufs=2)
         for h in range(2):
             for j in range(4):
                 nc.tensor.transpose(pad_bank[:, h, j, :], pad_cols[:, h, j : j + 1].to_broadcast([P, P]), ident_bf[:])
-        nc.scalar.activation(out=rest[:], in_=mask_bank[:, 0:TILES], func=ACT.Copy, scale=-1.0, bias=1.0)
-        nc.scalar.activation(out=keep_m[:], in_=mask_bank[:, 0:TILES], func=ACT.Copy)
+        mask_bank = psum.tile([P, P], BF16, name="mask_bank", tag="turned", bufs=2)
+        nc.tensor.transpose(mask_bank[:], mask_rows[:], ident_bf[:])
 
         def spread_pad(h):
             nc.scalar.activation(
@@ -272,10 +280,12 @@ def tile_length_masked_cross_keys_g6_kernel(tc, x_words, x_scales, w_key, mask, 
             )
 
         spread_pad(0)
-        for u in range(Q_HEAD):
-            make_q(u, True)
+        nc.scalar.activation(out=rest[:], in_=mask_bank[:, 0:TILES], func=ACT.Copy, scale=-1.0, bias=1.0)
+        nc.scalar.activation(out=keep_m[:], in_=mask_bank[:, 0:TILES], func=ACT.Copy)
         for g in range(PASSES):
-            if g == PASSES - 1 and HEAD_SPLIT < HALF:
+            for u in range(Q_BEFORE[g], Q_BEFORE[g + 1]):
+                make_q(u, True)
+            if g >= 2 and HEAD_SPLIT < HALF:
                 interleave_w(g, 0, 0, HALF // 2, False)
                 interleave_w(g, 0, HALF // 2, HEAD_SPLIT, False)
                 interleave_w(g, 0, HEAD_SPLIT, HALF, True)
@@ -286,7 +296,7 @@ def tile_length_masked_cross_keys_g6_kernel(tc, x_words, x_scales, w_key, mask, 
             quantize_w(g, 0, HALF // 2, HALF)
             for u in range(FIRST):
                 mx_pass(u, g)
-        for u in range(Q_HEAD, Q_AHEAD):
+        for u in range(Q_BEFORE[-1], Q_AHEAD):
             make_q(u, True)
         spread_pad(1)
 
@@ -301,7 +311,7 @@ def tile_length_masked_cross_keys_g6_kernel(tc, x_words, x_scales, w_key, mask, 
                 make_q(u + BATCH, False)
             if u < last:
                 round_y(u)
-            ahead = u + 4 if u + 4 < TILES else (u + AHEAD if u + AHEAD >= TILES else -1)
+            ahead = u + AHEAD0 if u + AHEAD0 < SWITCH else (u + AHEAD if u + AHEAD >= SWITCH else -1)
             if FIRST <= ahead < UNITS:
                 for g in range(PASSES):
                     mx_pass(ahead, g)
@@ -313,9 +323,9 @@ def tile_length_masked_cross_keys_g6_kernel(tc, x_words, x_scales, w_key, mask, 
                 unload(BATCH * UNLOAD_A.index(u), 2)
             if u in UNLOAD_B:
                 unload(BATCH * UNLOAD_B.index(u) + 2, 2)
-            if u % 2 == 1 and u < last:
+            if u % 2 == 1 and u < UNITS - 4:
                 store_y(u - 1, u + 1)
-            if u >= last - 1:
+            if u >= UNITS - 4:
                 store_y(u, u + 1)
             for at, g, c0, c1 in W1_SCALAR:
                 if at == u:
@@ -331,7 +341,9 @@ def tile_length_masked_cross_keys_g6_kernel(tc, x_words, x_scales, w_key, mask, 
                 quantize_y(BATCH * b, BATCH)
                 store_codes(BATCH * b, BATCH, nc.sync)
                 if BATCH * (b + 1) == TILES:
-                    store_scales(0, [nc.sync])
+                    store_scales(0, 0, [nc.sync])
+                if BATCH * (b + 1) == TILES + SCALE_CUT:
+                    store_scales(1, 0, [nc.sync])
             if u == last - 2:
                 quantize_y(UNITS - 2 * BATCH, 2)
             if u == last - 1:
@@ -350,4 +362,4 @@ def tile_length_masked_cross_keys_g6_kernel(tc, x_words, x_scales, w_key, mask, 
         store_codes(u0, 2, nc.sync)
         quantize_y(u0 + 3, 1)
         store_codes(u0 + 2, 2, nc.sync)
-        store_scales(1, [nc.scalar, nc.sync])
+        store_scales(1, SCALE_CUT, [nc.scalar, nc.sync])

@@ -39,8 +39,6 @@ UNLOAD_A = [5,9,13,17,21,24,27]
 UNLOAD_B = [6,10,14,18,21,24,27]
 QUANT_AT = [9,13,17,21,24,27]
 
-SCALE_CUT = 8
-
 FLOPS = 2 * TOKENS * D * C
 
 
@@ -113,11 +111,17 @@ def tile_length_masked_cross_keys_g6_kernel(tc, x_words, x_scales, w_key, mask, 
             h, i = divmod(u, TILES)
             if BATCH <= u < Q_AHEAD:
                 q_tiles[u] = keep.tile([P, HALF], F32, name="q_%d" % u, align_bytes=64)
+            elif u >= TILES and (u % 2 == 0 or False):
+                q_tiles[u] = flow.tile([P, HALF], F32, name="q_vector", tag="q_vector", bufs=6, align_bytes=64)
             else:
                 q_tiles[u] = flow.tile([P, HALF], F32, name="q", tag="q", bufs=BATCH, align_bytes=64)
             src = pad_rows[:, HALF * h : HALF * (h + 1)]
-            if on_scalar:
+            if on_scalar or (u >= TILES and False):
                 nc.scalar.activation(out=q_tiles[u][:], in_=src, func=ACT.Copy, scale=rest[:, i : i + 1])
+            elif u >= TILES and u % 2 == 0:
+                nc.vector.tensor_scalar(
+                    out=q_tiles[u][:], in0=src, scalar1=rest[:, i : i + 1], scalar2=None, op0=ALU.mult
+                )
             else:
                 nc.gpsimd.tensor_scalar(
                     out=q_tiles[u][:], in0=src, scalar1=rest[:, i : i + 1], scalar2=1.0, op0=ALU.mult, op1=ALU.mult
@@ -201,8 +205,7 @@ def tile_length_masked_cross_keys_g6_kernel(tc, x_words, x_scales, w_key, mask, 
         def quantize_y(u0, n):
             h, i = divmod(u0, TILES)
             b, j = divmod(u0, BATCH)
-            i0 = SCALE_CUT if h == 1 and i >= SCALE_CUT else 0
-            plane = y_scales[h, i0][:, P * (i - i0) : P * (i - i0 + n)]
+            plane = y_scales[h][4 * (i // BATCH) : P, P * j : P * (j + n)]
             nc.vector.quantize_mx(
                 out=y_codes[h][:, P * i : P * (i + n)].bitcast(FP8X4),
                 scales=plane,
@@ -214,12 +217,11 @@ def tile_length_masked_cross_keys_g6_kernel(tc, x_words, x_scales, w_key, mask, 
             dst = out_1[h].rearrange("p n t -> p (n t)").bitcast(I32)
             queue.dma_start(out=dst[:, P * i : P * (i + n)], in_=y_codes[h][:, P * i : P * (i + n)].bitcast(I32))
 
-        def store_scales(h, i0, queues):
-            tile = y_scales[h, i0]
+        def store_scales(h, queues):
             for quad in range(4):
+                dst = out_2[h, 4 * quad : 4 * quad + 4, :].rearrange("r (k n) -> k r n", k=4)
                 queues[quad % len(queues)].dma_start(
-                    out=out_2[h, 4 * quad : 4 * quad + 4, P * i0 : P * i0 + tile.shape[1]].bitcast(I32),
-                    in_=tile[32 * quad : 32 * quad + 4, :].bitcast(I32),
+                    out=dst.bitcast(I32), in_=y_scales[h][32 * quad : 32 * quad + 16, :].bitcast(I32)
                 )
 
         xs_first = keep.tile([P, PASSES, P * FIRST], U8, align_bytes=64)
@@ -232,31 +234,29 @@ def tile_length_masked_cross_keys_g6_kernel(tc, x_words, x_scales, w_key, mask, 
         rest = keep.tile([P, TILES], F32, align_bytes=64)
         pad_rows = keep.tile([P, C], F32, align_bytes=64)
         y_codes = [keep.tile([P, TOKENS], U32, name="y_codes_%d" % h, align_bytes=64) for h in range(2)]
-        y_scales = {}
-        for h, i0, i1 in ((0, 0, TILES), (1, 0, SCALE_CUT), (1, SCALE_CUT, TILES)):
-            y_scales[h, i0] = keep.tile([P, P * (i1 - i0)], U8, name="y_scales_%d_%d" % (h, i0), align_bytes=64)
+        y_scales = [keep.tile([P, CHUNK], U8, name="y_scales_%d" % h, align_bytes=64) for h in range(2)]
 
         nc.vector.memset(mask_rows[:], 0.0)
         nc.vector.memset(xs_first[:].bitcast(U32), 0)
         nc.vector.memset(x_planes[:].bitcast(U32), 0)
         make_identity(nc, ident_bf[:])
-        nc.gpsimd.dma_start(out=mask_rows[0:TILES, :], in_=mask.rearrange("b (i p) -> (b i) p", p=P))
-        for quad in (0, 2, 1, 3):
-            nc.gpsimd.dma_start(
-                out=x_planes[32 * quad : 32 * quad + 4 * PASSES, :].bitcast(I32),
-                in_=x_scales[:, 4 * quad : 4 * quad + 4, P * FIRST : TOKENS].bitcast(I32),
-            )
 
         load_w(0, 0)
         nc.scalar.dma_start(out=pad_cols[:], in_=pad_key.rearrange("(h p j) -> p h j", h=2, j=4))
+        nc.scalar.dma_start(out=mask_rows[0:TILES, :], in_=mask.rearrange("b (i p) -> (b i) p", p=P))
         for quad in (0, 2, 1, 3):
             src = x_scales[:, 4 * quad : 4 * quad + 4, 0 : P * FIRST].rearrange("g r n -> r g n")
             nc.sync.dma_start(out=xs_first[32 * quad : 32 * quad + 4, :, :].bitcast(I32), in_=src.bitcast(I32))
-        load_x_first(0)
         load_w(1, 0)
+        load_x_first(0)
         load_w(2, 0)
         load_x_first(1)
         load_x_first(2)
+        for quad in (0, 2, 1, 3):
+            nc.sync.dma_start(
+                out=x_planes[32 * quad : 32 * quad + 4 * PASSES, :].bitcast(I32),
+                in_=x_scales[:, 4 * quad : 4 * quad + 4, P * FIRST : TOKENS].bitcast(I32),
+            )
         load_x(1)
         load_w(0, 1)
         load_x(2)
@@ -341,9 +341,7 @@ def tile_length_masked_cross_keys_g6_kernel(tc, x_words, x_scales, w_key, mask, 
                 quantize_y(BATCH * b, BATCH)
                 store_codes(BATCH * b, BATCH, nc.sync)
                 if BATCH * (b + 1) == TILES:
-                    store_scales(0, 0, [nc.sync])
-                if BATCH * (b + 1) == TILES + SCALE_CUT:
-                    store_scales(1, 0, [nc.sync])
+                    store_scales(0, [nc.sync])
             if u == last - 2:
                 quantize_y(UNITS - 2 * BATCH, 2)
             if u == last - 1:
@@ -362,4 +360,4 @@ def tile_length_masked_cross_keys_g6_kernel(tc, x_words, x_scales, w_key, mask, 
         store_codes(u0, 2, nc.sync)
         quantize_y(u0 + 3, 1)
         store_codes(u0 + 2, 2, nc.sync)
-        store_scales(1, SCALE_CUT, [nc.scalar, nc.sync])
+        store_scales(1, [nc.scalar, nc.sync])

@@ -14,30 +14,24 @@ ACT = mybir.ActivationFunctionType
 
 P = 128
 TOKENS, D, C = 2048, 1536, 1024
-PASSES = D // 512
+K_PASS = 4 * P
+PASSES = D // K_PASS
 HALF = 512
 TILES = TOKENS // P
 UNITS = 2 * TILES
 BATCH = 4
-CHUNK = BATCH * P
-LAG = 3
-Q_AHEAD = 10
-Q_BEFORE = [0,0,0,5]
-X_BOUNDS = [0,5,9,13,16]
-FIRST = X_BOUNDS[1]
-W1_VECTOR = [[6,0,256,512],[8,1,0,256],[10,2,0,256]]
-W1_SCALAR = [[2,0,0,256],[5,1,256,512],[8,2,256,512]]
-W1_QUANT = [[7,0],[9,1],[11,2]]
-HEAD_SPLIT = 512
-QLAG = 2
+BATCHES = UNITS // BATCH
+ACC_BANKS = 6
+TURN_BANKS = 2
+QUADRANTS = (0, 2, 1, 3)
 
+FIRST = 5
 AHEAD = 2
-AHEAD0 = 3
-SWITCH = 22
-TURN_AT = [8,12,16,20,23,26,29]
-UNLOAD_A = [5,9,13,17,21,24,27]
-UNLOAD_B = [6,10,14,18,21,24,27]
-QUANT_AT = [9,13,17,21,24,27]
+EARLY_LAG = 5
+QUANT_DELAY = 4
+PAD_HEAD = 11
+W_SCALAR = 2
+W_VECTOR = 7
 
 FLOPS = 2 * TOKENS * D * C
 
@@ -45,6 +39,9 @@ FLOPS = 2 * TOKENS * D * C
 def tile_length_masked_cross_keys_g6_kernel(tc, x_words, x_scales, w_key, mask, pad_key, out_0, out_1, out_2):
     nc = tc.nc
     y_rows = out_0.rearrange("b t c -> (b t) c")
+    x_hbm = x_words.rearrange("g p n t -> p g (n t)").bitcast(I32)
+    last = UNITS - 1
+    end = UNITS - BATCH
 
     with ExitStack() as ctx:
         keep = ctx.enter_context(tc.tile_pool(name="keep", bufs=1))
@@ -52,50 +49,29 @@ def tile_length_masked_cross_keys_g6_kernel(tc, x_words, x_scales, w_key, mask, 
         psum = ctx.enter_context(tc.psum_pool(name="psum", bufs=1))
         ctx.enter_context(tc.manual_schedule())
 
-        w_raw = {}
-        w_grouped = {}
-        w_codes = {}
-        w_scales = {}
-        x_codes = {}
-        q_tiles = {}
-        acc = {}
-        y_tiles = {}
-        y_bf = {}
-        turned = {}
-        y_grouped = {}
+        w_raw, w_grouped, w_codes, w_scales = {}, {}, {}, {}
+        x_codes, pad_term, acc = {}, {}, {}
+        y_pair, y_bf, turned, y_grouped = {}, {}, {}, {}
 
         def load_w(g, h):
             w_raw[g, h] = keep.tile([P, 4, HALF], BF16, name="w_raw_%d_%d" % (g, h), align_bytes=64)
-            rows = w_key[512 * g : 512 * (g + 1), HALF * h : HALF * (h + 1)]
-            nc.sync.dma_start(out=w_raw[g, h][:], in_=rows.rearrange("(p j) c -> p j c", j=4))
+            rows = w_key[K_PASS * g : K_PASS * (g + 1), HALF * h : HALF * (h + 1)]
+            nc.sync.dma_start(out=w_raw[g, h][:], in_=rows.rearrange("(p t) c -> p t c", t=4))
 
-        def x_view(g):
-            return x_words[g].rearrange("p n t -> p (n t)").bitcast(I32)
-
-        def load_x_first(g):
-            t = keep.tile([P, P * FIRST], U32, name="x_first_%d" % g, align_bytes=64)
-            nc.sync.dma_start(out=t[:].bitcast(I32), in_=x_view(g)[:, 0 : P * FIRST])
-            for i in range(FIRST):
-                x_codes[g, i] = t[:, P * i : P * (i + 1)]
-
-        def load_x(k):
-            i0, i1 = X_BOUNDS[k], X_BOUNDS[k + 1]
-            t = keep.tile([P, PASSES, P * (i1 - i0)], U32, name="x_chunk_%d" % k, align_bytes=64)
-            src = x_words.rearrange("g p n t -> p g (n t)").bitcast(I32)
-            nc.sync.dma_start(out=t[:].bitcast(I32), in_=src[:, :, P * i0 : P * i1])
-            for g in range(PASSES):
+        def load_x(g0, g1, i0, i1):
+            words = keep.tile([P, g1 - g0, P * (i1 - i0)], U32, name="x_%d_%d" % (g0, i0), align_bytes=64)
+            nc.sync.dma_start(out=words[:].bitcast(I32), in_=x_hbm[:, g0:g1, P * i0 : P * i1])
+            for g in range(g0, g1):
                 for i in range(i0, i1):
-                    x_codes[g, i] = t[:, g, P * (i - i0) : P * (i - i0 + 1)]
+                    x_codes[g, i] = words[:, g - g0, P * (i - i0) : P * (i - i0 + 1)]
 
-        def interleave_w(g, h, c0, c1, on_scalar):
+        def interleave_w(g, h, c0, c1, copy):
             if (g, h) not in w_grouped:
                 w_grouped[g, h] = flow.tile([P, 4 * HALF], BF16, name="w_grouped", tag="w_grouped", bufs=3, align_bytes=64)
-            dst = w_grouped[g, h][:, 4 * c0 : 4 * c1].rearrange("p (c i t) -> p c t i", i=4, t=4)
-            src = w_raw[g, h][:, :, c0:c1].rearrange("p t (c i) -> p c t i", i=4)
-            if on_scalar:
-                nc.scalar.copy(out=dst, in_=src)
-            else:
-                nc.vector.tensor_copy(out=dst, in_=src)
+            copy(
+                out=w_grouped[g, h][:, 4 * c0 : 4 * c1].rearrange("p (c i t) -> p c t i", i=4, t=4),
+                in_=w_raw[g, h][:, :, c0:c1].rearrange("p t (c i) -> p c t i", i=4),
+            )
 
         def quantize_w(g, h, c0, c1):
             if c0 == 0:
@@ -107,38 +83,39 @@ def tile_length_masked_cross_keys_g6_kernel(tc, x_words, x_scales, w_key, mask, 
                 in_=w_grouped[g, h][:, 4 * c0 : 4 * c1],
             )
 
-        def make_q(u, on_scalar):
+        def spread_pad(h):
+            nc.scalar.activation(
+                out=pad_rows[:, HALF * h : HALF * (h + 1)].rearrange("p (n j) -> p n j", j=4),
+                in_=pad_bank[:, h, :, :].rearrange("p j n -> p n j"),
+                func=ACT.Copy,
+            )
+
+        def make_pad_term(u):
             h, i = divmod(u, TILES)
-            if BATCH <= u < Q_AHEAD:
-                q_tiles[u] = keep.tile([P, HALF], F32, name="q_%d" % u, align_bytes=64)
-            elif u >= TILES and (u % 2 == 0 or False):
-                q_tiles[u] = flow.tile([P, HALF], F32, name="q_vector", tag="q_vector", bufs=6, align_bytes=64)
+            if BATCH <= u < PAD_HEAD:
+                pad_term[u] = keep.tile([P, HALF], F32, name="pad_term_%d" % u, align_bytes=64)
             else:
-                q_tiles[u] = flow.tile([P, HALF], F32, name="q", tag="q", bufs=BATCH, align_bytes=64)
-            src = pad_rows[:, HALF * h : HALF * (h + 1)]
-            if on_scalar or (u >= TILES and False):
-                nc.scalar.activation(out=q_tiles[u][:], in_=src, func=ACT.Copy, scale=rest[:, i : i + 1])
-            elif u >= TILES and u % 2 == 0:
-                nc.vector.tensor_scalar(
-                    out=q_tiles[u][:], in0=src, scalar1=rest[:, i : i + 1], scalar2=None, op0=ALU.mult
-                )
+                pad_term[u] = flow.tile([P, HALF], F32, name="pad_term", tag="pad_term", bufs=BATCH, align_bytes=64)
+            pad_half = pad_rows[:, HALF * h : HALF * (h + 1)]
+            if u < PAD_HEAD:
+                nc.scalar.activation(out=pad_term[u][:], in_=pad_half, func=ACT.Copy, scale=mask_rest[:, i : i + 1])
             else:
                 nc.gpsimd.tensor_scalar(
-                    out=q_tiles[u][:], in0=src, scalar1=rest[:, i : i + 1], scalar2=1.0, op0=ALU.mult, op1=ALU.mult
+                    out=pad_term[u][:], in0=pad_half, scalar1=mask_rest[:, i : i + 1], scalar2=1.0, op0=ALU.mult, op1=ALU.mult
                 )
 
         def mx_pass(u, g):
             h, i = divmod(u, TILES)
             if g == 0:
-                acc[u] = psum.tile([P, HALF], F32, name="acc", tag="acc", bufs=6)
+                acc[u] = psum.tile([P, HALF], F32, name="acc", tag="acc", bufs=ACC_BANKS)
             if i < FIRST:
-                plane = xs_first[:, g, P * i : P * (i + 1)]
+                x_plane = x_planes_first[:, g, P * i : P * (i + 1)]
             else:
-                plane = x_planes[4 * g : P, P * (i - FIRST) : P * (i - FIRST + 1)]
+                x_plane = x_planes_rest[4 * g : P, P * (i - FIRST) : P * (i - FIRST + 1)]
             nc.tensor.matmul_mx(
                 out=acc[u][:],
                 lhsT=x_codes[g, i].bitcast(FP8X4),
-                lhsT_scale=plane,
+                lhsT_scale=x_plane,
                 rhs=w_codes[g, h][:].bitcast(FP8X4),
                 rhs_scale=w_scales[g, h][:],
                 start=(g == 0),
@@ -146,56 +123,55 @@ def tile_length_masked_cross_keys_g6_kernel(tc, x_words, x_scales, w_key, mask, 
             )
 
         def blend(u):
-            h, i = divmod(u, TILES)
             if u % 2 == 0:
-                y_tiles[u // 2] = flow.tile([P, 2, HALF], F32, name="y", tag="y", bufs=12, align_bytes=64)
+                y_pair[u // 2] = flow.tile([P, 2, HALF], F32, name="y_pair", tag="y_pair", bufs=12, align_bytes=64)
             nc.vector.scalar_tensor_tensor(
-                out=y_tiles[u // 2][:, u % 2, :],
+                out=y_pair[u // 2][:, u % 2, :],
                 in0=acc[u][:],
-                scalar=keep_m[:, i : i + 1],
-                in1=q_tiles[u][:],
+                scalar=mask_cols[:, u % TILES : u % TILES + 1],
+                in1=pad_term[u][:],
                 op0=ALU.mult,
                 op1=ALU.add,
             )
 
-        def store_y(u0, u1):
+        def store_y(u0, n):
             h, i = divmod(u0, TILES)
-            n = u1 - u0
             dst = y_rows[P * i : P * (i + n), HALF * h : HALF * (h + 1)].rearrange("(i p) c -> p i c", p=P)
-            nc.sync.dma_start(out=dst, in_=y_tiles[u0 // 2][:, u0 % 2 : u0 % 2 + n, :])
+            nc.sync.dma_start(out=dst, in_=y_pair[u0 // 2][:, u0 % 2 : u0 % 2 + n, :])
 
-        def round_y(u):
+        def new_y_bf(u):
             y_bf[u] = flow.tile([P, HALF], BF16, name="y_bf", tag="y_bf", bufs=12, align_bytes=64)
-            nc.scalar.copy(
+
+        def round_y(u, copy):
+            new_y_bf(u)
+            copy(
                 out=y_bf[u][:].rearrange("p (s c e) -> p s c e", s=2, e=2),
-                in_=y_tiles[u // 2][:, u % 2, :].rearrange("p (c s e) -> p s c e", s=2, e=2),
+                in_=y_pair[u // 2][:, u % 2, :].rearrange("p (c s e) -> p s c e", s=2, e=2),
             )
 
         def blend_rounded(u):
-            h, i = divmod(u, TILES)
-            y_bf[u] = flow.tile([P, HALF], BF16, name="y_bf", tag="y_bf", bufs=12, align_bytes=64)
+            new_y_bf(u)
             for s in range(2):
                 nc.vector.scalar_tensor_tensor(
                     out=y_bf[u][:, 2 * P * s : 2 * P * (s + 1)].rearrange("p (c e) -> p c e", e=2),
                     in0=acc[u][:].rearrange("p (c s e) -> p s c e", s=2, e=2)[:, s],
-                    scalar=keep_m[:, i : i + 1],
-                    in1=q_tiles[u][:].rearrange("p (c s e) -> p s c e", s=2, e=2)[:, s],
+                    scalar=mask_cols[:, u % TILES : u % TILES + 1],
+                    in1=pad_term[u][:].rearrange("p (c s e) -> p s c e", s=2, e=2)[:, s],
                     op0=ALU.mult,
                     op1=ALU.add,
                 )
 
         def turn(u0, n, tag, bufs):
-            bank = psum.tile([P, n, 2, P], F32, name="turned", tag=tag, bufs=bufs)
-            turned[u0] = bank
+            turned[u0] = psum.tile([P, n, 2, P], F32, name="turned", tag=tag, bufs=bufs)
             for a in range(n):
-                words = y_bf[u0 + a][:].bitcast(F32)
+                pairs = y_bf[u0 + a][:].bitcast(F32)
                 for s in range(2):
-                    nc.tensor.transpose(bank[:, a, s, :], words[:, P * s : P * (s + 1)], ident_f32[:])
+                    nc.tensor.transpose(turned[u0][:, a, s, :], pairs[:, P * s : P * (s + 1)], ident_f32[:])
 
         def unload(u0, n):
             b, j = divmod(u0, BATCH)
             if j == 0:
-                y_grouped[b] = flow.tile([P, 4 * CHUNK], BF16, name="y_grouped", tag="y_grouped", bufs=4, align_bytes=64)
+                y_grouped[b] = flow.tile([P, 4 * P * BATCH], BF16, name="y_grouped", tag="y_grouped", bufs=4, align_bytes=64)
             dst = y_grouped[b][:, 4 * P * j : 4 * P * (j + n)].bitcast(F32)
             nc.scalar.copy(
                 out=dst.rearrange("p (a m s) -> p a m s", a=n, s=2),
@@ -205,159 +181,146 @@ def tile_length_masked_cross_keys_g6_kernel(tc, x_words, x_scales, w_key, mask, 
         def quantize_y(u0, n):
             h, i = divmod(u0, TILES)
             b, j = divmod(u0, BATCH)
-            plane = y_scales[h][4 * (i // BATCH) : P, P * j : P * (j + n)]
             nc.vector.quantize_mx(
                 out=y_codes[h][:, P * i : P * (i + n)].bitcast(FP8X4),
-                scales=plane,
+                scales=y_planes[h][4 * (i // BATCH) : P, P * j : P * (j + n)],
                 in_=y_grouped[b][:, 4 * P * j : 4 * P * (j + n)],
             )
 
-        def store_codes(u0, n, queue):
+        def store_codes(u0, n):
             h, i = divmod(u0, TILES)
             dst = out_1[h].rearrange("p n t -> p (n t)").bitcast(I32)
-            queue.dma_start(out=dst[:, P * i : P * (i + n)], in_=y_codes[h][:, P * i : P * (i + n)].bitcast(I32))
+            nc.sync.dma_start(out=dst[:, P * i : P * (i + n)], in_=y_codes[h][:, P * i : P * (i + n)].bitcast(I32))
 
         def store_scales(h, queues):
             for quad in range(4):
                 dst = out_2[h, 4 * quad : 4 * quad + 4, :].rearrange("r (k n) -> k r n", k=4)
                 queues[quad % len(queues)].dma_start(
-                    out=dst.bitcast(I32), in_=y_scales[h][32 * quad : 32 * quad + 16, :].bitcast(I32)
+                    out=dst.bitcast(I32), in_=y_planes[h][32 * quad : 32 * quad + 16, :].bitcast(I32)
                 )
 
-        xs_first = keep.tile([P, PASSES, P * FIRST], U8, align_bytes=64)
-        x_planes = keep.tile([P, TOKENS - P * FIRST], U8, align_bytes=64)
+        x_planes_first = keep.tile([P, PASSES, P * FIRST], U8, align_bytes=64)
+        x_planes_rest = keep.tile([P, TOKENS - P * FIRST], U8, align_bytes=64)
         mask_rows = keep.tile([P, P], BF16, align_bytes=64)
         pad_cols = keep.tile([P, 2, 4], BF16, align_bytes=64)
         ident_bf = keep.tile([P, P], BF16, align_bytes=64)
         ident_f32 = keep.tile([P, P], F32, align_bytes=64)
-        keep_m = keep.tile([P, TILES], F32, align_bytes=64)
-        rest = keep.tile([P, TILES], F32, align_bytes=64)
+        mask_cols = keep.tile([P, TILES], F32, align_bytes=64)
+        mask_rest = keep.tile([P, TILES], F32, align_bytes=64)
         pad_rows = keep.tile([P, C], F32, align_bytes=64)
         y_codes = [keep.tile([P, TOKENS], U32, name="y_codes_%d" % h, align_bytes=64) for h in range(2)]
-        y_scales = [keep.tile([P, CHUNK], U8, name="y_scales_%d" % h, align_bytes=64) for h in range(2)]
+        y_planes = [keep.tile([P, P * BATCH], U8, name="y_planes_%d" % h, align_bytes=64) for h in range(2)]
 
         nc.vector.memset(mask_rows[:], 0.0)
-        nc.vector.memset(xs_first[:].bitcast(U32), 0)
-        nc.vector.memset(x_planes[:].bitcast(U32), 0)
+        nc.vector.memset(x_planes_first[:].bitcast(U32), 0)
+        nc.vector.memset(x_planes_rest[:].bitcast(U32), 0)
         make_identity(nc, ident_bf[:])
 
-        load_w(0, 0)
         nc.scalar.dma_start(out=pad_cols[:], in_=pad_key.rearrange("(h p j) -> p h j", h=2, j=4))
         nc.scalar.dma_start(out=mask_rows[0:TILES, :], in_=mask.rearrange("b (i p) -> (b i) p", p=P))
-        for quad in (0, 2, 1, 3):
+        load_w(0, 0)
+        for quad in QUADRANTS:
             src = x_scales[:, 4 * quad : 4 * quad + 4, 0 : P * FIRST].rearrange("g r n -> r g n")
-            nc.sync.dma_start(out=xs_first[32 * quad : 32 * quad + 4, :, :].bitcast(I32), in_=src.bitcast(I32))
+            nc.sync.dma_start(out=x_planes_first[32 * quad : 32 * quad + 4, :, :].bitcast(I32), in_=src.bitcast(I32))
+        load_x(0, 1, 0, FIRST)
         load_w(1, 0)
-        load_x_first(0)
         load_w(2, 0)
-        load_x_first(1)
-        load_x_first(2)
-        for quad in (0, 2, 1, 3):
+        load_x(1, 2, 0, FIRST)
+        load_x(2, 3, 0, FIRST)
+        for quad in QUADRANTS:
             nc.sync.dma_start(
-                out=x_planes[32 * quad : 32 * quad + 4 * PASSES, :].bitcast(I32),
+                out=x_planes_rest[32 * quad : 32 * quad + 4 * PASSES, :].bitcast(I32),
                 in_=x_scales[:, 4 * quad : 4 * quad + 4, P * FIRST : TOKENS].bitcast(I32),
             )
-        load_x(1)
+        load_x(0, PASSES, FIRST, FIRST + BATCH)
         load_w(0, 1)
-        load_x(2)
+        load_x(0, PASSES, FIRST + BATCH, FIRST + 2 * BATCH)
         load_w(1, 1)
         load_w(2, 1)
-        load_x(3)
+        load_x(0, PASSES, FIRST + 2 * BATCH, TILES)
 
         nc.scalar.activation(out=ident_f32[:], in_=ident_bf[:], func=ACT.Copy)
-        pad_bank = psum.tile([P, 2, 4, P], BF16, name="pad_bank", tag="turned", bufs=2)
+        pad_bank = psum.tile([P, 2, 4, P], BF16, name="pad_bank", tag="turned", bufs=TURN_BANKS)
         for h in range(2):
             for j in range(4):
                 nc.tensor.transpose(pad_bank[:, h, j, :], pad_cols[:, h, j : j + 1].to_broadcast([P, P]), ident_bf[:])
-        mask_bank = psum.tile([P, P], BF16, name="mask_bank", tag="turned", bufs=2)
+        mask_bank = psum.tile([P, P], BF16, name="mask_bank", tag="turned", bufs=TURN_BANKS)
         nc.tensor.transpose(mask_bank[:], mask_rows[:], ident_bf[:])
-
-        def spread_pad(h):
-            nc.scalar.activation(
-                out=pad_rows[:, HALF * h : HALF * (h + 1)].rearrange("p (n j) -> p n j", j=4),
-                in_=pad_bank[:, h, :, :].rearrange("p j n -> p n j"),
-                func=ACT.Copy,
-            )
-
         spread_pad(0)
-        nc.scalar.activation(out=rest[:], in_=mask_bank[:, 0:TILES], func=ACT.Copy, scale=-1.0, bias=1.0)
-        nc.scalar.activation(out=keep_m[:], in_=mask_bank[:, 0:TILES], func=ACT.Copy)
+        nc.scalar.activation(out=mask_rest[:], in_=mask_bank[:, 0:TILES], func=ACT.Copy, scale=-1.0, bias=1.0)
+        nc.scalar.activation(out=mask_cols[:], in_=mask_bank[:, 0:TILES], func=ACT.Copy)
+        for u in range(PAD_HEAD):
+            make_pad_term(u)
+        spread_pad(1)
+
         for g in range(PASSES):
-            for u in range(Q_BEFORE[g], Q_BEFORE[g + 1]):
-                make_q(u, True)
-            if g >= 2 and HEAD_SPLIT < HALF:
-                interleave_w(g, 0, 0, HALF // 2, False)
-                interleave_w(g, 0, HALF // 2, HEAD_SPLIT, False)
-                interleave_w(g, 0, HEAD_SPLIT, HALF, True)
-            else:
-                interleave_w(g, 0, 0, HALF // 2, False)
-                interleave_w(g, 0, HALF // 2, HALF, False)
+            interleave_w(g, 0, 0, HALF // 2, nc.vector.tensor_copy)
+            interleave_w(g, 0, HALF // 2, HALF, nc.vector.tensor_copy)
             quantize_w(g, 0, 0, HALF // 2)
             quantize_w(g, 0, HALF // 2, HALF)
             for u in range(FIRST):
                 mx_pass(u, g)
-        for u in range(Q_BEFORE[-1], Q_AHEAD):
-            make_q(u, True)
-        spread_pad(1)
 
-        last = UNITS - 1
+        turn_step = []
+        for b in range(BATCHES - 1):
+            lag = min(EARLY_LAG, AHEAD + BATCHES - 2 - b)
+            turn_step.append(BATCH * b + BATCH - 1 + lag - AHEAD)
+        quant_step = [step + QUANT_DELAY for step in turn_step[:-1]]
+
         for u in range(UNITS):
             if u == last:
                 blend_rounded(u)
             blend(u)
             if u < BATCH:
-                make_q(u + Q_AHEAD, False)
-            elif Q_AHEAD <= u < UNITS - BATCH:
-                make_q(u + BATCH, False)
-            if u < last:
-                round_y(u)
-            ahead = u + AHEAD0 if u + AHEAD0 < SWITCH else (u + AHEAD if u + AHEAD >= SWITCH else -1)
-            if FIRST <= ahead < UNITS:
+                make_pad_term(u + PAD_HEAD)
+            elif PAD_HEAD <= u < end:
+                make_pad_term(u + BATCH)
+            if u == end + 1:
+                round_y(end, nc.vector.tensor_copy)
+            if u != end and u != last:
+                round_y(u, nc.scalar.copy)
+            if FIRST <= u + AHEAD < UNITS:
                 for g in range(PASSES):
-                    mx_pass(ahead, g)
-            if ahead in TURN_AT:
-                b = TURN_AT.index(ahead)
-                turn(BATCH * b, 2, "turned", 2)
-                turn(BATCH * b + 2, 2, "turned", 2)
-            if u in UNLOAD_A:
-                unload(BATCH * UNLOAD_A.index(u), 2)
-            if u in UNLOAD_B:
-                unload(BATCH * UNLOAD_B.index(u) + 2, 2)
-            if u % 2 == 1 and u < UNITS - 4:
-                store_y(u - 1, u + 1)
-            if u >= UNITS - 4:
-                store_y(u, u + 1)
-            for at, g, c0, c1 in W1_SCALAR:
-                if at == u:
-                    interleave_w(g, 1, c0, c1, True)
-            for at, g, c0, c1 in W1_VECTOR:
-                if at == u:
-                    interleave_w(g, 1, c0, c1, False)
-            for at, g in W1_QUANT:
-                if at == u:
+                    mx_pass(u + AHEAD, g)
+            if u in turn_step:
+                u0 = BATCH * turn_step.index(u)
+                turn(u0, 2, "turned", TURN_BANKS)
+                turn(u0 + 2, 2, "turned", TURN_BANKS)
+                unload(u0, 2)
+                unload(u0 + 2, 2)
+            if u >= end:
+                store_y(u, 1)
+            elif u % 2 == 1:
+                store_y(u - 1, 2)
+            for g in range(PASSES):
+                if u == W_SCALAR + 3 * g:
+                    interleave_w(g, 1, HALF // 2, HALF, nc.scalar.copy)
+                if u == W_VECTOR + 2 * g:
+                    interleave_w(g, 1, 0, HALF // 2, nc.vector.tensor_copy)
+                if u == W_VECTOR + 2 * g + 1:
                     quantize_w(g, 1, 0, HALF)
-            if u in QUANT_AT:
-                b = QUANT_AT.index(u)
+            if u in quant_step:
+                b = quant_step.index(u)
                 quantize_y(BATCH * b, BATCH)
-                store_codes(BATCH * b, BATCH, nc.sync)
+                if b % 2 == 1:
+                    store_codes(BATCH * (b - 1), 2 * BATCH)
                 if BATCH * (b + 1) == TILES:
                     store_scales(0, [nc.sync])
             if u == last - 2:
-                quantize_y(UNITS - 2 * BATCH, 2)
+                quantize_y(end - BATCH, 2)
             if u == last - 1:
-                quantize_y(UNITS - 2 * BATCH + 2, 2)
-                store_codes(UNITS - 2 * BATCH, BATCH, nc.sync)
+                quantize_y(end - 2, 2)
+                store_codes(end - BATCH, BATCH)
 
-        u0 = UNITS - BATCH
-        turn(u0, 2, "turned", 2)
-        turn(u0 + 2, 1, "turned", 2)
-        turn(u0 + 3, 1, "acc", 6)
-        unload(u0, 2)
-        unload(u0 + 2, 1)
-        unload(u0 + 3, 1)
-        quantize_y(u0, 2)
-        quantize_y(u0 + 2, 1)
-        store_codes(u0, 2, nc.sync)
-        quantize_y(u0 + 3, 1)
-        store_codes(u0 + 2, 2, nc.sync)
+        turn(end, 2, "turned", TURN_BANKS)
+        turn(end + 2, 1, "turned", TURN_BANKS)
+        turn(last, 1, "acc", ACC_BANKS)
+        unload(end, 2)
+        unload(end + 2, 1)
+        unload(last, 1)
+        quantize_y(end, 2)
+        quantize_y(end + 2, 1)
+        store_codes(end, 2)
+        quantize_y(last, 1)
+        store_codes(end + 2, 2)
         store_scales(1, [nc.scalar, nc.sync])

from contextlib import ExitStack

import concourse.mybir as mybir
from concourse.masks import make_identity

F32 = mybir.dt.float32
BF16 = mybir.dt.bfloat16
I32 = mybir.dt.int32
U32 = mybir.dt.uint32
U8 = mybir.dt.uint8
FP8X4 = mybir.dt.float8_e4m3fn_x4
ALU = mybir.AluOpType
ACT = mybir.ActivationFunctionType

P = 128
TOKENS, D, C = 2048, 1536, 1024
K_PASS = 4 * P
PASSES = D // K_PASS
HALF = 512
TILES = TOKENS // P
UNITS = 2 * TILES
BATCH = 4
BATCHES = UNITS // BATCH
ACC_BANKS = 6
TURN_BANKS = 2
QUADRANTS = (0, 2, 1, 3)

FIRST = 5
AHEAD = 2
EARLY_LAG = 5
QUANT_DELAY = 4
PAD_HEAD = 11
W_SCALAR = 2
W_VECTOR = 7

FLOPS = 2 * TOKENS * D * C


def tile_length_masked_cross_keys_g6_kernel(tc, x_words, x_scales, w_key, mask, pad_key, out_0, out_1, out_2):
    nc = tc.nc
    y_rows = out_0.rearrange("b t c -> (b t) c")
    x_hbm = x_words.rearrange("g p n t -> p g (n t)").bitcast(I32)
    last = UNITS - 1
    end = UNITS - BATCH

    with ExitStack() as ctx:
        keep = ctx.enter_context(tc.tile_pool(name="keep", bufs=1))
        flow = ctx.enter_context(tc.tile_pool(name="flow", bufs=1))
        psum = ctx.enter_context(tc.psum_pool(name="psum", bufs=1))
        ctx.enter_context(tc.manual_schedule())

        w_raw, w_grouped, w_codes, w_scales = {}, {}, {}, {}
        x_codes, pad_term, acc = {}, {}, {}
        y_pair, y_bf, turned, y_grouped = {}, {}, {}, {}

        def load_w(g, h):
            w_raw[g, h] = keep.tile([P, 4, HALF], BF16, name="w_raw_%d_%d" % (g, h), align_bytes=64)
            rows = w_key[K_PASS * g : K_PASS * (g + 1), HALF * h : HALF * (h + 1)]
            nc.sync.dma_start(out=w_raw[g, h][:], in_=rows.rearrange("(p t) c -> p t c", t=4))

        def load_x(g0, g1, i0, i1):
            words = keep.tile([P, g1 - g0, P * (i1 - i0)], U32, name="x_%d_%d" % (g0, i0), align_bytes=64)
            nc.sync.dma_start(out=words[:].bitcast(I32), in_=x_hbm[:, g0:g1, P * i0 : P * i1])
            for g in range(g0, g1):
                for i in range(i0, i1):
                    x_codes[g, i] = words[:, g - g0, P * (i - i0) : P * (i - i0 + 1)]

        def interleave_w(g, h, c0, c1, copy):
            if (g, h) not in w_grouped:
                w_grouped[g, h] = flow.tile([P, 4 * HALF], BF16, name="w_grouped", tag="w_grouped", bufs=3, align_bytes=64)
            copy(
                out=w_grouped[g, h][:, 4 * c0 : 4 * c1].rearrange("p (c i t) -> p c t i", i=4, t=4),
                in_=w_raw[g, h][:, :, c0:c1].rearrange("p t (c i) -> p c t i", i=4),
            )

        def quantize_w(g, h, c0, c1):
            if c0 == 0:
                w_codes[g, h] = keep.tile([P, HALF], U32, name="w_codes_%d_%d" % (g, h), align_bytes=64)
                w_scales[g, h] = keep.tile([P, HALF], U8, name="w_scales_%d_%d" % (g, h), align_bytes=64)
            nc.vector.quantize_mx(
                out=w_codes[g, h][:, c0:c1].bitcast(FP8X4),
                scales=w_scales[g, h][:, c0:c1],
                in_=w_grouped[g, h][:, 4 * c0 : 4 * c1],
            )

        def spread_pad(h):
            nc.scalar.activation(
                out=pad_rows[:, HALF * h : HALF * (h + 1)].rearrange("p (n j) -> p n j", j=4),
                in_=pad_bank[:, h, :, :].rearrange("p j n -> p n j"),
                func=ACT.Copy,
            )

        def make_pad_term(u):
            h, i = divmod(u, TILES)
            if BATCH <= u < PAD_HEAD:
                pad_term[u] = keep.tile([P, HALF], F32, name="pad_term_%d" % u, align_bytes=64)
            else:
                pad_term[u] = flow.tile([P, HALF], F32, name="pad_term", tag="pad_term", bufs=BATCH, align_bytes=64)
            pad_half = pad_rows[:, HALF * h : HALF * (h + 1)]
            if u < PAD_HEAD:
                nc.scalar.activation(out=pad_term[u][:], in_=pad_half, func=ACT.Copy, scale=mask_rest[:, i : i + 1])
            else:
                nc.gpsimd.tensor_scalar(
                    out=pad_term[u][:], in0=pad_half, scalar1=mask_rest[:, i : i + 1], scalar2=1.0, op0=ALU.mult, op1=ALU.mult
                )

        def mx_pass(u, g):
            h, i = divmod(u, TILES)
            if g == 0:
                acc[u] = psum.tile([P, HALF], F32, name="acc", tag="acc", bufs=ACC_BANKS)
            if i < FIRST:
                x_plane = x_planes_first[:, g, P * i : P * (i + 1)]
            else:
                x_plane = x_planes_rest[4 * g : P, P * (i - FIRST) : P * (i - FIRST + 1)]
            nc.tensor.matmul_mx(
                out=acc[u][:],
                lhsT=x_codes[g, i].bitcast(FP8X4),
                lhsT_scale=x_plane,
                rhs=w_codes[g, h][:].bitcast(FP8X4),
                rhs_scale=w_scales[g, h][:],
                start=(g == 0),
                stop=(g == PASSES - 1),
            )

        def blend(u):
            if u % 2 == 0:
                y_pair[u // 2] = flow.tile([P, 2, HALF], F32, name="y_pair", tag="y_pair", bufs=12, align_bytes=64)
            nc.vector.scalar_tensor_tensor(
                out=y_pair[u // 2][:, u % 2, :],
                in0=acc[u][:],
                scalar=mask_cols[:, u % TILES : u % TILES + 1],
                in1=pad_term[u][:],
                op0=ALU.mult,
                op1=ALU.add,
            )

        def store_y(u0, n):
            h, i = divmod(u0, TILES)
            dst = y_rows[P * i : P * (i + n), HALF * h : HALF * (h + 1)].rearrange("(i p) c -> p i c", p=P)
            nc.sync.dma_start(out=dst, in_=y_pair[u0 // 2][:, u0 % 2 : u0 % 2 + n, :])

        def new_y_bf(u):
            y_bf[u] = flow.tile([P, HALF], BF16, name="y_bf", tag="y_bf", bufs=12, align_bytes=64)

        def round_y(u, copy):
            new_y_bf(u)
            copy(
                out=y_bf[u][:].rearrange("p (s c e) -> p s c e", s=2, e=2),
                in_=y_pair[u // 2][:, u % 2, :].rearrange("p (c s e) -> p s c e", s=2, e=2),
            )

        def blend_rounded(u):
            new_y_bf(u)
            for s in range(2):
                nc.vector.scalar_tensor_tensor(
                    out=y_bf[u][:, 2 * P * s : 2 * P * (s + 1)].rearrange("p (c e) -> p c e", e=2),
                    in0=acc[u][:].rearrange("p (c s e) -> p s c e", s=2, e=2)[:, s],
                    scalar=mask_cols[:, u % TILES : u % TILES + 1],
                    in1=pad_term[u][:].rearrange("p (c s e) -> p s c e", s=2, e=2)[:, s],
                    op0=ALU.mult,
                    op1=ALU.add,
                )

        def turn(u0, n, tag, bufs):
            turned[u0] = psum.tile([P, n, 2, P], F32, name="turned", tag=tag, bufs=bufs)
            for a in range(n):
                pairs = y_bf[u0 + a][:].bitcast(F32)
                for s in range(2):
                    nc.tensor.transpose(turned[u0][:, a, s, :], pairs[:, P * s : P * (s + 1)], ident_f32[:])

        def unload(u0, n):
            b, j = divmod(u0, BATCH)
            if j == 0:
                y_grouped[b] = flow.tile([P, 4 * P * BATCH], BF16, name="y_grouped", tag="y_grouped", bufs=4, align_bytes=64)
            dst = y_grouped[b][:, 4 * P * j : 4 * P * (j + n)].bitcast(F32)
            nc.scalar.copy(
                out=dst.rearrange("p (a m s) -> p a m s", a=n, s=2),
                in_=turned[u0][:].rearrange("p a s m -> p a m s"),
            )

        def quantize_y(u0, n):
            h, i = divmod(u0, TILES)
            b, j = divmod(u0, BATCH)
            nc.vector.quantize_mx(
                out=y_codes[h][:, P * i : P * (i + n)].bitcast(FP8X4),
                scales=y_planes[h][4 * (i // BATCH) : P, P * j : P * (j + n)],
                in_=y_grouped[b][:, 4 * P * j : 4 * P * (j + n)],
            )

        def store_codes(u0, n):
            h, i = divmod(u0, TILES)
            dst = out_1[h].rearrange("p n t -> p (n t)").bitcast(I32)
            nc.sync.dma_start(out=dst[:, P * i : P * (i + n)], in_=y_codes[h][:, P * i : P * (i + n)].bitcast(I32))

        def store_scales(h, queues):
            for quad in range(4):
                dst = out_2[h, 4 * quad : 4 * quad + 4, :].rearrange("r (k n) -> k r n", k=4)
                queues[quad % len(queues)].dma_start(
                    out=dst.bitcast(I32), in_=y_planes[h][32 * quad : 32 * quad + 16, :].bitcast(I32)
                )

        x_planes_first = keep.tile([P, PASSES, P * FIRST], U8, align_bytes=64)
        x_planes_rest = keep.tile([P, TOKENS - P * FIRST], U8, align_bytes=64)
        mask_rows = keep.tile([P, P], BF16, align_bytes=64)
        pad_cols = keep.tile([P, 2, 4], BF16, align_bytes=64)
        ident_bf = keep.tile([P, P], BF16, align_bytes=64)
        ident_f32 = keep.tile([P, P], F32, align_bytes=64)
        mask_cols = keep.tile([P, TILES], F32, align_bytes=64)
        mask_rest = keep.tile([P, TILES], F32, align_bytes=64)
        pad_rows = keep.tile([P, C], F32, align_bytes=64)
        y_codes = [keep.tile([P, TOKENS], U32, name="y_codes_%d" % h, align_bytes=64) for h in range(2)]
        y_planes = [keep.tile([P, P * BATCH], U8, name="y_planes_%d" % h, align_bytes=64) for h in range(2)]

        nc.vector.memset(mask_rows[:], 0.0)
        nc.vector.memset(x_planes_first[:].bitcast(U32), 0)
        nc.vector.memset(x_planes_rest[:].bitcast(U32), 0)
        make_identity(nc, ident_bf[:])

        nc.scalar.dma_start(out=pad_cols[:], in_=pad_key.rearrange("(h p j) -> p h j", h=2, j=4))
        nc.scalar.dma_start(out=mask_rows[0:TILES, :], in_=mask.rearrange("b (i p) -> (b i) p", p=P))
        load_w(0, 0)
        for quad in QUADRANTS:
            src = x_scales[:, 4 * quad : 4 * quad + 4, 0 : P * FIRST].rearrange("g r n -> r g n")
            nc.sync.dma_start(out=x_planes_first[32 * quad : 32 * quad + 4, :, :].bitcast(I32), in_=src.bitcast(I32))
        load_x(0, 1, 0, FIRST)
        load_w(1, 0)
        load_w(2, 0)
        load_x(1, 2, 0, FIRST)
        load_x(2, 3, 0, FIRST)
        for quad in QUADRANTS:
            nc.sync.dma_start(
                out=x_planes_rest[32 * quad : 32 * quad + 4 * PASSES, :].bitcast(I32),
                in_=x_scales[:, 4 * quad : 4 * quad + 4, P * FIRST : TOKENS].bitcast(I32),
            )
        load_x(0, PASSES, FIRST, FIRST + BATCH)
        load_w(0, 1)
        load_x(0, PASSES, FIRST + BATCH, FIRST + 2 * BATCH)
        load_w(1, 1)
        load_w(2, 1)
        load_x(0, PASSES, FIRST + 2 * BATCH, TILES)

        nc.scalar.activation(out=ident_f32[:], in_=ident_bf[:], func=ACT.Copy)
        pad_bank = psum.tile([P, 2, 4, P], BF16, name="pad_bank", tag="turned", bufs=TURN_BANKS)
        for h in range(2):
            for j in range(4):
                nc.tensor.transpose(pad_bank[:, h, j, :], pad_cols[:, h, j : j + 1].to_broadcast([P, P]), ident_bf[:])
        mask_bank = psum.tile([P, P], BF16, name="mask_bank", tag="turned", bufs=TURN_BANKS)
        nc.tensor.transpose(mask_bank[:], mask_rows[:], ident_bf[:])
        spread_pad(0)
        nc.scalar.activation(out=mask_rest[:], in_=mask_bank[:, 0:TILES], func=ACT.Copy, scale=-1.0, bias=1.0)
        nc.scalar.activation(out=mask_cols[:], in_=mask_bank[:, 0:TILES], func=ACT.Copy)
        for u in range(PAD_HEAD):
            make_pad_term(u)
        spread_pad(1)

        for g in range(PASSES):
            interleave_w(g, 0, 0, HALF // 2, nc.vector.tensor_copy)
            interleave_w(g, 0, HALF // 2, HALF, nc.vector.tensor_copy)
            quantize_w(g, 0, 0, HALF // 2)
            quantize_w(g, 0, HALF // 2, HALF)
            for u in range(FIRST):
                mx_pass(u, g)

        turn_step = []
        for b in range(BATCHES - 1):
            lag = min(EARLY_LAG, AHEAD + BATCHES - 2 - b)
            turn_step.append(BATCH * b + BATCH - 1 + lag - AHEAD)
        quant_step = [step + QUANT_DELAY for step in turn_step[:-1]]

        for u in range(UNITS):
            if u == last:
                blend_rounded(u)
            blend(u)
            if u < BATCH:
                make_pad_term(u + PAD_HEAD)
            elif PAD_HEAD <= u < end:
                make_pad_term(u + BATCH)
            if u == end + 1:
                round_y(end, nc.vector.tensor_copy)
            if u != end and u != last:
                round_y(u, nc.scalar.copy)
            if FIRST <= u + AHEAD < UNITS:
                for g in range(PASSES):
                    mx_pass(u + AHEAD, g)
            if u in turn_step:
                u0 = BATCH * turn_step.index(u)
                turn(u0, 2, "turned", TURN_BANKS)
                turn(u0 + 2, 2, "turned", TURN_BANKS)
                unload(u0, 2)
                unload(u0 + 2, 2)
            if u >= end:
                store_y(u, 1)
            elif u % 2 == 1:
                store_y(u - 1, 2)
            for g in range(PASSES):
                if u == W_SCALAR + 3 * g:
                    interleave_w(g, 1, HALF // 2, HALF, nc.scalar.copy)
                if u == W_VECTOR + 2 * g:
                    interleave_w(g, 1, 0, HALF // 2, nc.vector.tensor_copy)
                if u == W_VECTOR + 2 * g + 1:
                    quantize_w(g, 1, 0, HALF)
            if u in quant_step:
                b = quant_step.index(u)
                quantize_y(BATCH * b, BATCH)
                if b % 2 == 1:
                    store_codes(BATCH * (b - 1), 2 * BATCH)
                if BATCH * (b + 1) == TILES:
                    store_scales(0, [nc.sync])
            if u == last - 2:
                quantize_y(end - BATCH, 2)
            if u == last - 1:
                quantize_y(end - 2, 2)
                store_codes(end - BATCH, BATCH)

        turn(end, 2, "turned", TURN_BANKS)
        turn(end + 2, 1, "turned", TURN_BANKS)
        turn(last, 1, "acc", ACC_BANKS)
        unload(end, 2)
        unload(end + 2, 1)
        unload(last, 1)
        quantize_y(end, 2)
        quantize_y(end + 2, 1)
        store_codes(end, 2)
        quantize_y(last, 1)
        store_codes(end + 2, 2)
        store_scales(1, [nc.scalar, nc.sync])
